import numpy as np, ml_dtypes
CORES = [2,3,42,43,82,83,122,123]
N = 8
BF = ml_dtypes.bfloat16
V, CAP, LB, RO = 2048, 128, 2, 3
L = N * V
PL = (np.arange(N)[:, None] * V + np.arange(V)).reshape(N, 1, 1, V)
def draw(rng, size):
    s = (N, 8, 16, V)
    t = PL + 1 + (size * rng.random(s) * rng.random(s)).astype(np.int64)
    t = np.where(t > L, np.minimum(PL + 1 + ((L - PL) * rng.random(s)).astype(np.int64), L), t); z = rng.random(s)
    return np.where(z < 0.12, 0, np.where(z < 0.121, L, t))
def sizes(rng):
    a = np.array([V >> 6, V >> 5, V >> 4, V >> 3, V >> 3, V >> 2, V >> 1, 2 * V])[rng.permutation(8)]
    return (a[:, None] * np.exp2(2 * rng.random((8, 16)) - 1)).reshape(1, 8, 16, 1)
def perms(rng):
    return np.argsort(rng.random((N, 8, 16, LB)), axis=2)
def pack(t, rt):
    return {"ends": np.ascontiguousarray(t.reshape(N, 128, V)).astype(np.int32), "rights": np.ascontiguousarray(rt.reshape(N, 128, LB)).astype(np.int32)}
def setup_inputs(rng):
    return pack(draw(rng, sizes(rng)), perms(rng))
def setup_inputs_room(rng):
    t = draw(rng, np.full((1, 8, 16, 1), V >> 4)); p = np.arange(V)
    for r in range(N):
        for g in range(8):
            for b in range(LB):
                v = np.where((p == V - 1) | (rng.random(V) < 0.3), 0, r * V + p + 1 + ((V - 1 - p) * rng.random(V)).astype(np.int64))
                o = rng.permutation(V); k = 0
                for q in range(r + 1, N):
                    n = int(rng.choice(np.array([0, 1, CAP - 1, CAP, CAP + 1, 2 * CAP])))
                    if r == 0 and q == 1 and b == 0: n = (CAP, CAP + 1, 2 * CAP, CAP - 1, 1, 0, CAP, CAP + 1)[g]
                    x = rng.integers(0, V, n)
                    if n > 1: x[0] = 0; x[n - 1] = V - 1
                    v[o[k:k + n]] = q * V + x; k += n
                t[r, g, b] = v
    return pack(t, perms(rng))
def setup_inputs_alike(rng):
    t = draw(rng, sizes(rng)); p = PL.reshape(-1)
    for g in (0, 2, 4, 6):
        s = np.array([V, 1, 16, V // 4] * 4)
        if g: s = s[rng.permutation(16)]
        t[:, g] = np.minimum((PL[:, 0] // s[None, :, None] + 1) * s[None, :, None], L)
    for g in (1, 3):
        for a in range(16):
            cut = np.append(np.sort(rng.integers(1, L, 40)), L)
            t[:, g, a] = cut[np.searchsorted(cut, p, side="right")].reshape(N, V)
    rt = rng.integers(0, 16, (N, 8, 16, LB)); rt[:, 0] = np.arange(LB); rt[:, 2] = rng.choice(np.array([0, 15]), (N, 16, LB))
    return pack(t, rt)
def setup_inputs_fails(rng):
    t = draw(rng, sizes(rng)); rt = perms(rng); q = 1 + rng.permutation(7); h = V // 2; e = (N - 1) * V
    t[rng.integers(0, N), :, :LB] = 0
    t[:, 0, :LB] = 0; t[:, q[0], :LB] = 0; t[:, q[1], :LB] = L
    t[:, q[2]] = np.where(rng.random((N, 1, V)) < 0.6, 0, t[:, q[2]]); t[:, q[3], LB:] = 0
    b = int(rng.integers(0, LB))
    t[:, q[4], b] = np.where(rng.random((N, V)) < 0.1, L, 0); rt[:, q[4], b] = rng.integers(LB, 16, (N, LB))
    for s in (q[5], q[6]):
        t[:N - 1, s, :LB] = 0; t[N - 1, s, :, :h] = 0; t[N - 1, s, 0, :h] = e + h + rng.integers(0, h, h)
        for r in range(N - 1):
            o = rng.permutation(V)[:CAP]; t[r, s, 0, o] = e + rng.integers(0, h, CAP)
        rt[:N - 1, s, :, 0] = rng.integers(1, 15, (N - 1, 16))
    t[N - 1, q[6], 15, :h] = L; rt[:N - 1, q[6], 0, 0] = 15
    return pack(t, rt)
def setup_inputs_far(rng):
    t = draw(rng, np.full((1, 8, 16, 1), 8 * L))
    t[:, :, :LB] = np.where(rng.random((N, 8, LB, V)) < 0.85, 0, t[:, :, :LB])
    for r in range(N - 1):
        o = rng.permutation(8)
        for q in range(r + 1, N):
            b = int(rng.integers(1, LB)); v = np.where(rng.random(V) < 0.04, L, q * V + rng.integers(0, V, V))
            t[r, o[q], b] = v; t[r, o[q], 0] = np.where(rng.random(V) < 0.04, v, t[r, o[q], 0])
    t[:, :, :LB, 0] = L - 1; t[:, :, :LB, V - 1] = ((np.arange(N) + 1) * V)[:, None, None]
    return pack(t, perms(rng))
def setup_inputs_spread(rng):
    u = rng.random((N, 8, 16, V)) * np.sqrt(rng.random((N, 8, 1, V)))
    t = np.minimum(PL + np.maximum(np.exp2(np.log2(L - PL) * u).astype(np.int64), 1), L)
    t = np.where(rng.random(t.shape) < rng.random((N, 8, 1, 1)) * 0.3, 0, t)
    return pack(t, rng.integers(0, 16, (N, 8, 16, LB)))
def check_inputs(d):
    bad = []; a = np.asarray(d["ends"]).astype(np.int64); b = np.asarray(d["rights"])
    if not np.all((a == 0) | ((a > PL.reshape(N, 1, V)) & (a <= L))): bad.append("range of ends")
    if np.min(b) < 0 or np.max(b) > 15: bad.append("range of rights")
    return bad
def reference(ends, rights):
    m = np.ascontiguousarray(ends.astype(np.int64).reshape(N, 8, 16, V).transpose(1, 2, 0, 3)).reshape(8, 16, L)
    rt = rights.astype(np.int64).reshape(N, 8, 16, LB).transpose(1, 2, 0, 3)
    own = (np.arange(L) // V)[None, :]
    for rnd in range(RO):
        new = m
        for b in range(LB):
            t = m[:, b]; good = (t > 0) & (t < L); to = np.where(good, t // V, N)
            for q in range(1, N):
                far = (to == q) & (own < q)
                h = far.reshape(8, N, V).astype(np.int64); before = np.add.accumulate(h, axis=2) - h
                good = good & ~(far & (before.reshape(8, L) >= CAP))
            c = np.take_along_axis(m, np.where(good, t, 0)[:, None, :], 2)
            c = np.where(good[:, None, :], c, 0)
            c = np.take_along_axis(c.reshape(8, 16, N, V), rt[:, :, :, b:b + 1], 1).reshape(8, 16, L)
            new = np.maximum(new, c)
        m = new
    return {"y": np.ascontiguousarray(m.reshape(8, 16, N, V).transpose(2, 0, 1, 3)).reshape(N, 128, V).astype(np.float32)}

@@ -1,0 +1,367 @@
+import numpy as np
+from concourse.bass import DstId, RemoteDMATransfer
+from concourse.mybir import AluOpType, ActivationFunctionType
+
+V, N, RO, CAP = 2048, 8, 3, 128
+SEG = CAP + 1
+LOC = 8
+BLK = LOC + V
+BW = 136
+WCOLS = BLK + 9 * BW
+LCOLS = V + 7 * CAP
+CHUNKS = 4
+ROUND_C = 1.5 * 2.0 ** 34
+
+SCRATCH = {
+    "ei": ("sbuf", [128, V], "int32"), "E0": ("sbuf", [128, V], "float32"), "E1": ("sbuf", [128, V], "float32"),
+    "win0": ("sbuf", [128, WCOLS], "float32"), "win1": ("sbuf", [128, WCOLS], "float32"),
+    "wl0": ("sbuf", [128, LCOLS], "float32"), "wl1": ("sbuf", [128, LCOLS], "float32"),
+    "ri": ("sbuf", [128, 2], "int32"), "rf": ("sbuf", [128, 2], "float32"), "rcol": ("sbuf", [128, 2], "float32"),
+    "iom": ("sbuf", [128, 128], "float32"), "iop": ("sbuf", [128, 1], "float32"), "iosx": ("sbuf", [128, 16], "float32"),
+    "ip32": ("sbuf", [128, 1], "int32"), "im32": ("sbuf", [128, 128], "int32"),
+    "p16i": ("sbuf", [128, 1], "int32"), "p15i": ("sbuf", [128, 1], "int32"),
+    "p16f": ("sbuf", [128, 1], "float32"), "p15f": ("sbuf", [128, 1], "float32"),
+    "mm": ("sbuf", [128, 128], "int32"), "mg": ("sbuf", [128, 128], "float32"), "tg": ("sbuf", [128, 128], "float32"),
+    "idf": ("sbuf", [128, 128], "float32"), "id128": ("sbuf", [128, 128], "float32"), "selx": ("sbuf", [128, 16], "float32"),
+    "idb": ("sbuf", [128, 128], "bfloat16"), "wa": ("sbuf", [128, 128], "bfloat16"), "wb": ("sbuf", [128, 128], "bfloat16"),
+    "xi": ("sbuf", [128, 128], "float32"), "d0": ("sbuf", [128, 7 * SEG], "bfloat16"),
+    "oh0": ("sbuf", [128, 7 * SEG], "bfloat16"), "oh1": ("sbuf", [128, 7 * SEG], "bfloat16"),
+    "sc0": ("sbuf", [128, 7 * SEG], "bfloat16"), "sc1": ("sbuf", [128, 7 * SEG], "bfloat16"),
+    "rl0": ("sbuf", [128, 7 * CAP], "bfloat16"), "rl1": ("sbuf", [128, 7 * CAP], "bfloat16"),
+    "roh": ("sbuf", [128, 256], "float32"), "sr": ("sbuf", [128, 256], "float32"),
+    "xs": ("sbuf", [128, 256], "float32"), "qb": ("sbuf", [128, 256], "bfloat16"), "rqv": ("sbuf", [128, 256], "float32"),
+    "yv": ("sbuf", [128, 256], "float32"), "zv": ("sbuf", [128, 256], "float32"), "o16": ("sbuf", [128, 256], "uint16"),
+    "u1": ("sbuf", [128, 256], "float32"), "a1": ("sbuf", [128, 256], "float32"),
+    "si": ("sbuf", [128, 256], "int32"), "av": ("sbuf", [128, 256], "float32"), "a16": ("sbuf", [128, 256], "uint16"),
+    "lq": ("sbuf", [128, 7 * 16], "float32"), "lo": ("sbuf", [128, 7 * 16], "uint16"),
+    "rp": ("sbuf", [128, 7 * 256], "uint16"), "ld": ("sbuf", [128, 7 * 256], "uint16"), "ldf": ("sbuf", [128, 7 * 256], "float32"),
+    "rqb": ("dram", [7, 128, 16], "float32"), "rland": ("dram", [7, 128, 16], "float32"),
+}
+for _k in range(8):
+    SCRATCH["ps%d" % _k] = ("psum", [128, 512], "float32")
+SEMAPHORES = (["qV", "qT", "qS", "qG", "lri", "dq0", "dq1", "lsq", "st0", "st1", "st2", "st3"] + ["le%d" % k for k in range(CHUNKS)]
+              + ["rq%d" % k for k in range(7)] + ["rp%d" % k for k in range(8)] + ["ls%d" % k for k in range(7)] + ["lw%d" % k for k in range(7)])
+
+ADD, SUB, MUL, MAX, MIN, EQ, GT = (AluOpType.add, AluOpType.subtract, AluOpType.mult, AluOpType.max, AluOpType.min,
+                                   AluOpType.is_equal, AluOpType.is_gt)
+ACT = ActivationFunctionType
+
+
+def rank_program(g, core, T, topo):
+    r = T.rank_of(core)
+    if r is None:
+        return
+    cores = T.cores
+    later = list(range(r + 1, N))
+    nq, nr = len(later), r
+    Q = {"V": g.vector, "T": g.tensor, "S": g.scalar, "Y": g.sync, "G": g}
+    total, clock, snap, acc, bank = {}, {q: {} for q in Q}, {}, {}, {}
+
+    def need(q, sem, val):
+        ck = clock[q]
+        if ck.get(sem, 0) >= val:
+            return
+        Q[q].wait_ge(T.sem[sem], val)
+        ck[sem] = val
+        for k, v in snap.get((sem, val), {}).items():
+            if ck.get(k, 0) < v:
+                ck[k] = v
+
+    def order(q, reads, writes, banks, extra):
+        want = {}
+
+        def add(tok):
+            if want.get(tok[0], 0) < tok[1]:
+                want[tok[0]] = tok[1]
+        for (b, lo, hi) in reads:
+            for e in acc.get(b, []):
+                if e[4] and e[0] < hi and lo < e[1]:
+                    add(e[2])
+        for (b, lo, hi) in writes:
+            for e in acc.get(b, []):
+                if e[0] < hi and lo < e[1]:
+                    add(e[2])
+        for k in banks:
+            for oq, tok in bank.get(k, {}).items():
+                if oq != q:
+                    add(tok)
+        for tok in extra:
+            add(tok)
+        for sem in sorted(want, key=lambda s: (s[0] != "q", s)):
+            need(q, sem, want[sem])
+
+    def note(q, tok, reads, writes, banks):
+        s = dict(clock[q])
+        s[tok[0]] = tok[1]
+        snap[tok] = s
+        for (b, lo, hi) in writes:
+            keep = [e for e in acc.get(b, []) if not (lo <= e[0] and e[1] <= hi)]
+            keep.append((lo, hi, tok, q, True))
+            acc[b] = keep
+        for (b, lo, hi) in reads:
+            keep = [e for e in acc.get(b, []) if e[4] or e[3] != q or (e[0], e[1]) != (lo, hi) or e[2][0] != tok[0]]
+            keep.append((lo, hi, tok, q, False))
+            acc[b] = keep
+        for k in banks:
+            bank.setdefault(k, {})[q] = tok
+
+    def op(q, fn, reads=(), writes=(), banks=(), extra=()):
+        order(q, reads, writes, banks, extra)
+        sem = "q" + q
+        total[sem] = total.get(sem, 0) + 1
+        fn(Q[q]).then_inc(T.sem[sem], 1)
+        note(q, (sem, total[sem]), reads, writes, banks)
+        return (sem, total[sem])
+
+    def dmas(q, sem, items, extra=()):
+        tok = (sem, total.get(sem, 0) + 16 * len(items))
+        total[sem] = tok[1]
+        for (o, i, rd, wr) in items:
+            order(q, rd, wr, (), extra)
+            Q[q].dma_start(o, i).then_inc(T.sem[sem], 16)
+        for (o, i, rd, wr) in items:
+            note(q, tok, rd, wr, ())
+        return tok
+
+    def tokens(sem, n):
+        total[sem] = total.get(sem, 0) + n
+        return (sem, total[sem])
+
+    def ps(k, lo, hi):
+        return T["ps%d" % k][:, lo:hi]
+
+    def rem_mask(engs):
+        m = 0
+        for e in engs:
+            m |= 1 << e
+        return m
+
+    far = [c for c in cores if c != core and topo.chip(c) != topo.chip(core)]
+    pool = topo.engines(core, far[0])
+
+    CW = V // CHUNKS
+    dmas("S", "lri", [(T.ri[:], T.rights[:], (), [("ri", 0, 2)])])
+    for k in range(CHUNKS):
+        lo, hi = k * CW, (k + 1) * CW
+        dmas("Y" if k % 2 == 0 else "S", "le%d" % k, [(T.ei[:, lo:hi], T.ends[:, lo:hi], (), [("ei", lo, hi)])])
+
+    def iota(name, pat, base, cm, lo, hi, f32=True):
+        if f32:
+            op("G", lambda e: e.iota(T[name][:, lo:hi], pat, base, cm, allow_small_or_imprecise_dtypes=True), (), [(name, lo, hi)])
+        else:
+            op("G", lambda e: e.iota(T[name][:, lo:hi], pat, base, cm), (), [(name, lo, hi)])
+    iota("iop", [[1, 1]], 0, 1, 0, 1)
+    iota("iosx", [[1, 2], [16, 8]], 0, 0, 0, 16)
+    iota("iom", [[1, 128]], 0, 0, 0, 128)
+    iota("ip32", [[1, 1]], 0, 1, 0, 1, False)
+    iota("im32", [[1, 128]], 0, 0, 0, 128, False)
+    iota("xi", [[16, 128]], 0, 0, 0, 128)
+    if nq:
+        for b in range(2):
+            iota("wl%d" % b, [[V, nq], [0, CAP]], V * (r + 1), 0, V, V + CAP * nq)
+
+    def ts(out, i, s1, s2, op0, op1, reads, writes, banks=(), q="V"):
+        if op1 is None:
+            return op(q, lambda e: e.tensor_scalar(out, i, s1, None, op0), reads, writes, banks)
+        return op(q, lambda e: e.tensor_scalar(out, i, s1, s2, op0, op1), reads, writes, banks)
+
+    def tt(out, i0, i1, o, reads, writes, banks=()):
+        return op("V", lambda e: e.tensor_tensor(out, i0, i1, o), reads, writes, banks)
+
+    def cp(out, i, reads, writes, banks=()):
+        return op("V", lambda e: e.tensor_copy(out, i), reads, writes, banks)
+
+    def R(name, lo=0, hi=1 << 20):
+        return (name, lo, min(hi, SCRATCH[name][1][-1]))
+
+    def mset(ap, val, wr):
+        op("V", lambda e: e.memset(ap, val), (), [wr])
+
+    ts(T.selx[:], T.iosx[:], T.iop[:], None, EQ, None, [R("iosx"), R("iop")], [R("selx")])
+    ts(T.idf[:], T.iom[:], T.iop[:], None, EQ, None, [R("iom"), R("iop")], [R("idf")])
+    cp(T.idb[:], T.idf[:], [R("idf")], [R("idb")])
+    ts(T.p16i[:], T.ip32[:], 112, None, AluOpType.bitwise_and, None, [R("ip32")], [R("p16i")])
+    ts(T.p15i[:], T.ip32[:], 15, None, AluOpType.bitwise_and, None, [R("ip32")], [R("p15i")])
+    cp(T.p16f[:], T.p16i[:], [R("p16i")], [R("p16f")])
+    cp(T.p15f[:], T.p15i[:], [R("p15i")], [R("p15f")])
+    if nq:
+        ts(T.mm[:], T.im32[:], 112, None, AluOpType.bitwise_and, None, [R("im32")], [R("mm")])
+        ts(T.tg[:], T.iom[:], T.iop[:], None, GT, None, [R("iom"), R("iop")], [R("tg")])
+        ts(T.mg[:], T.mm[:], T.p16f[:], None, EQ, None, [R("mm"), R("p16f")], [R("mg")])
+        ts(T.id128[:], T.idf[:], 128.0, None, MUL, None, [R("idf")], [R("id128")])
+        tt(T.tg[:], T.tg[:], T.mg[:], MUL, [R("tg"), R("mg")], [R("tg")])
+        tt(T.id128[:], T.id128[:], T.tg[:], SUB, [R("id128"), R("tg")], [R("id128")])
+        cp(T.wa[:], T.id128[:], [R("id128")], [R("wa")])
+        tt(T.mg[:], T.mg[:], T.id128[:], ADD, [R("mg"), R("id128")], [R("mg")])
+        ts(T.wb[:], T.mg[:], -1.0, None, MUL, None, [R("mg")], [R("wb")])
+        ts(T.xi[:], T.xi[:], T.p15f[:], None, ADD, None, [R("xi"), R("p15f")], [R("xi")])
+        mset(T.d0[:], 1.0, R("d0"))
+        mset(T.oh0[:, 0:7 * SEG:SEG], 0.0, R("oh0"))
+        mset(T.oh1[:, 0:7 * SEG:SEG], 0.0, R("oh1"))
+        mset(T.d0[:, 0:7 * SEG:SEG], 0.0, R("d0"))
+    WC = BLK + BW * (9 - r)
+    for k in range(CHUNKS):
+        lo, hi = k * CW, (k + 1) * CW
+        cp(T.E0[:, lo:hi], T.ei[:, lo:hi], [R("ei", lo, hi)], [R("E0", lo, hi)])
+
+    def late_constants():
+        for b in range(2):
+            w = "win%d" % b
+            mset(T[w][:, 0:LOC + 1], 0.0, R(w, 0, LOC + 1))
+            mset(T[w][:, BLK:WC], 0.0, R(w, BLK, WC))
+        cp(T.rf[:], T.ri[:], [R("ri")], [R("rf")])
+        ts(T.rcol[:], T.rf[:], T.p16f[:], None, ADD, None, [R("rf"), R("p16f")], [R("rcol")])
+        for b in range(2):
+            ts(T.roh[:, 128 * b:128 * b + 128], T.iom[:], T.rcol[:, b:b + 1], None, EQ, None, [R("iom"), R("rcol")], [R("roh", 128 * b, 128 * b + 128)])
+
+    for n in range(RO):
+        E, X = ("E0", "E1") if n % 2 == 0 else ("E1", "E0")
+        for i in range(16):
+            op("T", lambda e: e.matmul(T.ps0[:, i:256:16], T[E][:, i:V:16], T.selx[:], True, True), [R(E), R("selx")], (), [0])
+        ts(T.xs[:], ps(0, 0, 256), -1023.75, None, ADD, None, (), [R("xs")], [0])
+        for b in range(2):
+            op("T", lambda e: e.transpose(ps(1, 128 * b, 128 * b + 128), T.xs[:, 128 * b:128 * b + 128], T.idf[:]), [R("xs"), R("idf")], (), [1])
+        ts(T.qb[:], ps(1, 0, 256), ROUND_C, ROUND_C, ADD, SUB, (), [R("qb")], [1])
+        if nq:
+            na = min(4, nq)
+            for b in range(2):
+                oh, sc = "oh%d" % b, "sc%d" % b
+                for k, q in enumerate(later):
+                    ts(T[oh][:, k * SEG + 1:(k + 1) * SEG], T.qb[:, 128 * b:128 * b + 128], float(V * q), None, EQ, None,
+                       [R("qb")], [R(oh, k * SEG + 1, (k + 1) * SEG)])
+                op("V", lambda e: e.tensor_tensor_scan(T[sc][:, 0:nq * SEG], T.d0[:, 0:nq * SEG], T[oh][:, 0:nq * SEG], 0.0, MUL, ADD),
+                   [R(oh), R("d0")], [R(sc)])
+            ts(T.rqv[:], T.qb[:], 1.0 / 16, float(V - 1 - CAP * (r + 1)), MUL, ADD, [R("qb")], [R("rqv")])
+
+            def count(b, part):
+                sc, bk = "sc%d" % b, 2 + 2 * b + part
+                for k in (range(na) if part == 0 else range(na, nq)):
+                    lo = (k % 4) * CAP
+                    op("T", lambda e: e.matmul(ps(bk, lo, lo + CAP), T.wa[:], T[sc][:, k * SEG + 1:(k + 1) * SEG], True, False), [R(sc), R("wa")], (), [bk])
+                    op("T", lambda e: e.matmul(ps(bk, lo, lo + CAP), T.wb[:], T[sc][:, k * SEG:(k + 1) * SEG - 1], False, True), [R(sc), R("wb")], (), [bk])
+
+            def positive(b, part):
+                rl, bk = "rl%d" % b, 2 + 2 * b + part
+                lo, hi = (0, na * CAP) if part == 0 else (na * CAP, nq * CAP)
+                if hi == lo:
+                    return
+                if part == 0:
+                    op("S", lambda e: e.activation(T[rl][:, lo:hi], ps(bk, 0, hi - lo), ACT.Relu), (), [R(rl, lo, hi)], [bk])
+                else:
+                    ts(T[rl][:, lo:hi], ps(bk, 0, hi - lo), 0.0, None, MAX, None, (), [R(rl, lo, hi)], [bk])
+
+            def slots(b):
+                rl = "rl%d" % b
+                for k in range(nq):
+                    op("T", lambda e: e.matmul(ps(6 + b, 0, CAP), T.idb[:], T[rl][:, k * CAP:(k + 1) * CAP], k == 0, k == nq - 1),
+                       [R(rl, k * CAP, (k + 1) * CAP), R("idb")], (), [6 + b])
+
+            def places(b):
+                lo, hi = 128 * b, 128 * b + 128
+                ts(T.yv[:, lo:hi], ps(6 + b, 0, CAP), 4096.0, -1.0, MUL, ADD, (), [R("yv", lo, hi)], [6 + b])
+                tt(T.zv[:, lo:hi], ps(6 + b, 0, CAP), T.rqv[:, lo:hi], ADD, [R("rqv")], [R("zv", lo, hi)], [6 + b])
+                tt(T.zv[:, lo:hi], T.zv[:, lo:hi], T.yv[:, lo:hi], MIN, [R("zv", lo, hi), R("yv", lo, hi)], [R("zv", lo, hi)])
+                tt(T.zv[:, lo:hi], T.zv[:, lo:hi], T.xi[:], MAX, [R("zv", lo, hi), R("xi")], [R("zv", lo, hi)])
+                cp(T.o16[:, lo:hi], T.zv[:, lo:hi], [R("zv", lo, hi)], [R("o16", lo, hi)])
+
+            LH = V + CAP * nq
+            count(0, 0)
+            count(0, 1)
+            positive(0, 0)
+            positive(0, 1)
+            count(1, 0)
+            positive(1, 0)
+            slots(0)
+            count(1, 1)
+            places(0)
+            op("S", lambda e: e.activation(T.wl0[:, 0:LH].indirect(T.o16[:, 0:128]), T[E][:], ACT.Silu), [R(E), R("o16", 0, 128)], [R("wl0", 0, LH)])
+            positive(1, 1)
+            slots(1)
+            places(1)
+            op("V", lambda e: e.tensor_copy(T.wl1[:, 0:LH].indirect(T.o16[:, 128:256]), T[E][:]), [R(E), R("o16", 128, 256)], [R("wl1", 0, LH)])
+            before = [("lsq", total["lsq"])] if n else []
+            for b in range(2):
+                wl, items = "wl%d" % b, []
+                for k in range(nq):
+                    lo = V + CAP * k
+                    items.append((T.rqb[k, b::2, :], T[wl][b::16, lo:lo + CAP], [R(wl, lo, lo + CAP)], ()))
+                tok = dmas("S" if b == 0 else "Y", "dq%d" % b, items, before)
+                need("G", tok[0], tok[1])
+            outs = [c for c in (cores[q] for q in later) if c in far]
+            w = 1
+            while 2 * w * max(len(later), 1) <= len(pool):
+                w *= 2
+            transfers = []
+            for k, q in enumerate(later):
+                rid, pid, _s = topo.addr(cores[q])
+                transfers.append(RemoteDMATransfer(dst_ids=[DstId(rid=rid, pnc=pid)], dma_engine_mask=rem_mask(pool[k * w:(k + 1) * w]),
+                                                   remote_sem=T.sem["rq%d" % r], src=T.rqb[k], dst=T.rland[r], alu_op=0))
+            g.remote_dma_fused(transfers, local_sem=T.sem.lsq)
+            tokens("lsq", w * nq)
+        if n == 0:
+            late_constants()
+            for b in range(2):
+                op("T", lambda e: e.transpose(ps(0, 128 * b, 128 * b + 128), T.roh[:, 128 * b:128 * b + 128], T.idf[:]),
+                   [R("roh", 128 * b, 128 * b + 128), R("idf")], (), [0])
+            cp(T.sr[:], ps(0, 0, 256), (), [R("sr")], [0])
+        for b in range(2):
+            w = "win%d" % b
+            for k in range(4):
+                bk, lo = 2 + k, 512 * k
+                op("T", lambda e: e.matmul(ps(bk, 0, 512), T.sr[:, 128 * b:128 * b + 128], T[E][:, lo:lo + 512], True, True), [R("sr"), R(E, lo, lo + 512)], (), [bk])
+                s = 1 if (k == 0 and r == 0) else 0
+                op("S", lambda e: e.activation(T[w][:, LOC + lo + s:LOC + lo + 512], ps(bk, s, 512), ACT.Copy), (), [R(w, LOC + lo + s, LOC + lo + 512)], [bk])
+        ts(T.u1[:], T.qb[:], 8.0, 1023.75 - V * r - 8.0 * V * r + LOC + 1, MUL, ADD, [R("qb")], [R("u1")])
+        ts(T.a1[:], T.qb[:], 17.0 / 256, float(BLK + 1 - BW * r), MUL, ADD, [R("qb")], [R("a1")])
+        tt(T.u1[:], ps(1, 0, 256), T.u1[:], ADD, [R("u1")], [R("u1")], [1])
+        tt(T.u1[:], T.u1[:], T.a1[:], MIN, [R("u1"), R("a1")], [R("u1")])
+        if nq:
+            for b in range(2):
+                lo, hi = 128 * b, 128 * b + 128
+                ts(T.si[:, lo:hi], ps(6 + b, 0, CAP), -1.0, 129.0, ADD, MUL, (), [R("si", lo, hi)], [6 + b])
+            ts(T.si[:], T.si[:], 4, 127, AluOpType.arith_shift_right, AluOpType.bitwise_and, [R("si")], [R("si")])
+            tt(T.av[:], T.yv[:], T.si[:], MIN, [R("yv"), R("si")], [R("av")])
+            tt(T.av[:], T.av[:], T.u1[:], ADD, [R("av"), R("u1")], [R("av")])
+        else:
+            ts(T.av[:], T.u1[:], -1.0, None, ADD, None, [R("u1")], [R("av")])
+        cp(T.a16[:], T.av[:], [R("av")], [R("a16")])
+        for p in range(nr):
+            w = 1
+            while 2 * w * max(N - 1 - p, 1) <= 8:
+                w *= 2
+            arr = tokens("rq%d" % p, w)
+            c0 = 16 * p
+            dmas("Y", "lw%d" % p, [(T.lq[:, c0:c0 + 16], T.rland[p], (), [R("lq", c0, c0 + 16)])], [arr])
+            ts(T.lo[:, c0:c0 + 16], T.lq[:, c0:c0 + 16], 0.25 - V * r, None, ADD, None, [R("lq", c0, c0 + 16)], [R("lo", c0, c0 + 16)])
+            left = [("ls%d" % p, total["ls%d" % p])] if n else []
+            tok = op("V", lambda e: e.tensor_copy(T.rp[:, 256 * p:256 * p + 256], T[E][:, 0:V].indirect(T.lo[:, c0:c0 + 16])),
+                     [R(E), R("lo", c0, c0 + 16)], [R("rp", 256 * p, 256 * p + 256)], (), left)
+            need("G", tok[0], tok[1])
+            rid, pid, _s = topo.addr(cores[p])
+            k = r - p - 1
+            g.remote_dma(out_ap=T.ld[:, 256 * k:256 * k + 256], in_ap=T.rp[:, 256 * p:256 * p + 256], remote_sem=T.sem["rp%d" % r],
+                         local_sem=T.sem["ls%d" % p], pid=pid, routing_id=rid, dma_engine_mask=rem_mask(pool))
+            tokens("ls%d" % p, len(pool))
+        for k, q in enumerate(later):
+            arr = tokens("rp%d" % q, len(pool))
+            lo = 256 * k
+            op("V", lambda e: e.tensor_copy(T.ldf[:, lo:lo + 256], T.ld[:, lo:lo + 256]), (), [R("ldf", lo, lo + 256)], (), [arr])
+            bk = (0, 1, 6, 7)[k % 4]
+            for b in range(2):
+                op("T", lambda e: e.matmul(ps(bk, 128 * b, 128 * b + 128), T.sr[:, 128 * b:128 * b + 128], T.ldf[:, lo + b:lo + 256:2], True, True),
+                   [R("ldf", lo, lo + 256), R("sr")], (), [bk])
+            c0 = BLK + BW * (k + 1) + 1
+            for b in range(2):
+                w = "win%d" % b
+                op("S", lambda e: e.activation(T[w][:, c0:c0 + CAP], ps(bk, 128 * b, 128 * b + 128), ACT.Copy), (), [R(w, c0, c0 + CAP)], [bk])
+        op("V", lambda e: e.tensor_tensor(T[X][:], T.win0[:, 0:WC].indirect(T.a16[:, 0:128]), T[E][:], MAX),
+           [R("win0", 0, WC), R("a16"), R(E)], [R(X)])
+        pieces = 1 if n < RO - 1 else 4
+        for k in range(pieces):
+            lo, hi = k * V // pieces, (k + 1) * V // pieces
+            op("V", lambda e: e.tensor_tensor(T[X][:, lo:hi], T.win1[:, 0:WC].indirect(T.a16[:, 128 + lo // 16:128 + hi // 16]), T[X][:, lo:hi], MAX),
+               [R("win1", 0, WC), R("a16"), R(X, lo, hi)], [R(X, lo, hi)])
+            if n == RO - 1:
+                dmas("Y" if k % 2 == 0 else "S", "st%d" % k, [(T.y[:, lo:hi], T[X][:, lo:hi], [R(X, lo, hi)], ())])
+    for sem in sorted(total):
+        need("G", sem, total[sem])

@@ -4,17 +4,17 @@ from concourse.mybir import AluOpType, ActivationFunctionType
 
 V, N, RO, CAP = 2048, 8, 3, 128
 SEG = CAP + 1
-LOC = 8
-BLK = LOC + V
-BW = 136
+Z = 8
+BLK = Z + 2 * V
+BW = Z + 2 * CAP
 WCOLS = BLK + 9 * BW
 LCOLS = V + 7 * CAP
-CHUNKS = 4
+CHUNKS, PIECES = 4, 8
 ROUND_C = 1.5 * 2.0 ** 34
 
 SCRATCH = {
     "ei": ("sbuf", [128, V], "int32"), "E0": ("sbuf", [128, V], "float32"), "E1": ("sbuf", [128, V], "float32"),
-    "win0": ("sbuf", [128, WCOLS], "float32"), "win1": ("sbuf", [128, WCOLS], "float32"),
+    "xw": ("sbuf", [128, 256], "int32"), "win": ("sbuf", [128, WCOLS], "float32"),
     "wl0": ("sbuf", [128, LCOLS], "float32"), "wl1": ("sbuf", [128, LCOLS], "float32"),
     "ri": ("sbuf", [128, 2], "int32"), "rf": ("sbuf", [128, 2], "float32"), "rcol": ("sbuf", [128, 2], "float32"),
     "iom": ("sbuf", [128, 128], "float32"), "iop": ("sbuf", [128, 1], "float32"), "iosx": ("sbuf", [128, 16], "float32"),
@@ -28,23 +28,37 @@ SCRATCH = {
     "oh0": ("sbuf", [128, 7 * SEG], "bfloat16"), "oh1": ("sbuf", [128, 7 * SEG], "bfloat16"),
     "sc0": ("sbuf", [128, 7 * SEG], "bfloat16"), "sc1": ("sbuf", [128, 7 * SEG], "bfloat16"),
     "rl0": ("sbuf", [128, 7 * CAP], "bfloat16"), "rl1": ("sbuf", [128, 7 * CAP], "bfloat16"),
-    "roh": ("sbuf", [128, 256], "float32"), "sr": ("sbuf", [128, 256], "float32"),
+    "roh": ("sbuf", [128, 256], "float32"), "sr": ("sbuf", [128, 256], "float32"), "srb": ("sbuf", [128, 256], "bfloat16"),
+    "srl": ("sbuf", [128, 7 * 256], "bfloat16"), "srf": ("sbuf", [128, 7 * 256], "float32"),
     "xs": ("sbuf", [128, 256], "float32"), "qb": ("sbuf", [128, 256], "bfloat16"), "rqv": ("sbuf", [128, 256], "float32"),
     "yv": ("sbuf", [128, 256], "float32"), "zv": ("sbuf", [128, 256], "float32"), "o16": ("sbuf", [128, 256], "uint16"),
     "u1": ("sbuf", [128, 256], "float32"), "a1": ("sbuf", [128, 256], "float32"),
     "si": ("sbuf", [128, 256], "int32"), "av": ("sbuf", [128, 256], "float32"), "a16": ("sbuf", [128, 256], "uint16"),
-    "lq": ("sbuf", [128, 7 * 16], "float32"), "lo": ("sbuf", [128, 7 * 16], "uint16"),
-    "rp": ("sbuf", [128, 7 * 256], "uint16"), "ld": ("sbuf", [128, 7 * 256], "uint16"), "ldf": ("sbuf", [128, 7 * 256], "float32"),
+    "lq": ("sbuf", [128, 7 * 16], "float32"), "lo": ("sbuf", [128, 7 * 16], "uint16"), "rpf": ("sbuf", [128, 7 * 256], "float32"),
+    "rp": ("sbuf", [128, 7 * 256], "uint16"), "ld": ("sbuf", [128, 7 * 256], "uint16"),
     "rqb": ("dram", [7, 128, 16], "float32"), "rland": ("dram", [7, 128, 16], "float32"),
 }
 for _k in range(8):
     SCRATCH["ps%d" % _k] = ("psum", [128, 512], "float32")
-SEMAPHORES = (["qV", "qT", "qS", "qG", "lri", "dq0", "dq1", "lsq", "st0", "st1", "st2", "st3"] + ["le%d" % k for k in range(CHUNKS)]
+SEMAPHORES = (["qV", "qT", "qS", "qG", "lri", "lx0", "lx1", "dq0", "dq1", "lsq", "lss", "sra"]
+              + ["le%d" % k for k in range(CHUNKS)] + ["st%d" % k for k in range(PIECES)]
               + ["rq%d" % k for k in range(7)] + ["rp%d" % k for k in range(8)] + ["ls%d" % k for k in range(7)] + ["lw%d" % k for k in range(7)])
 
 ADD, SUB, MUL, MAX, MIN, EQ, GT = (AluOpType.add, AluOpType.subtract, AluOpType.mult, AluOpType.max, AluOpType.min,
                                    AluOpType.is_equal, AluOpType.is_gt)
 ACT = ActivationFunctionType
+
+
+def out_engines(topo, cores, q):
+    far = [c for c in cores if topo.chip(c) != topo.chip(cores[q])]
+    return topo.engines(cores[q], far[0])
+
+
+def width(topo, cores, p):
+    n, w = len(out_engines(topo, cores, p)), 1
+    while 2 * w * max(N - 1 - p, 1) <= n:
+        w *= 2
+    return w
 
 
 def rank_program(g, core, T, topo):
@@ -136,29 +150,35 @@ def rank_program(g, core, T, topo):
             m |= 1 << e
         return m
 
-    far = [c for c in cores if c != core and topo.chip(c) != topo.chip(core)]
-    pool = topo.engines(core, far[0])
+    def R(name, lo=0, hi=1 << 20):
+        return (name, lo, min(hi, SCRATCH[name][1][-1]))
+
+    pool = out_engines(topo, cores, r)
+
+    def to_later(src, dst, remote, local):
+        w, transfers = width(topo, cores, r), []
+        for k, q in enumerate(later):
+            rid, pid, _s = topo.addr(cores[q])
+            transfers.append(RemoteDMATransfer(dst_ids=[DstId(rid=rid, pnc=pid)], dma_engine_mask=rem_mask(pool[k * w:(k + 1) * w]),
+                                               remote_sem=T.sem[remote], src=src(k), dst=dst, alu_op=0))
+        g.remote_dma_fused(transfers, local_sem=T.sem[local])
+        tokens(local, w * nq)
 
     CW = V // CHUNKS
-    dmas("S", "lri", [(T.ri[:], T.rights[:], (), [("ri", 0, 2)])])
+    dmas("S", "lri", [(T.ri[:], T.rights[:], (), [R("ri")])])
+    for b in range(2):
+        dmas("Y" if b == 0 else "S", "lx%d" % b,
+             [(T.xw[:, 128 * b + 16 * s:128 * b + 16 * s + 16], T.ends[16 * s + b:16 * s + b + 1, :], (),
+               [R("xw", 128 * b + 16 * s, 128 * b + 16 * s + 16)]) for s in range(8)])
     for k in range(CHUNKS):
         lo, hi = k * CW, (k + 1) * CW
-        dmas("Y" if k % 2 == 0 else "S", "le%d" % k, [(T.ei[:, lo:hi], T.ends[:, lo:hi], (), [("ei", lo, hi)])])
+        dmas("Y" if k % 2 == 0 else "S", "le%d" % k, [(T.ei[:, lo:hi], T.ends[:, lo:hi], (), [R("ei", lo, hi)])])
 
     def iota(name, pat, base, cm, lo, hi, f32=True):
         if f32:
             op("G", lambda e: e.iota(T[name][:, lo:hi], pat, base, cm, allow_small_or_imprecise_dtypes=True), (), [(name, lo, hi)])
         else:
             op("G", lambda e: e.iota(T[name][:, lo:hi], pat, base, cm), (), [(name, lo, hi)])
-    iota("iop", [[1, 1]], 0, 1, 0, 1)
-    iota("iosx", [[1, 2], [16, 8]], 0, 0, 0, 16)
-    iota("iom", [[1, 128]], 0, 0, 0, 128)
-    iota("ip32", [[1, 1]], 0, 1, 0, 1, False)
-    iota("im32", [[1, 128]], 0, 0, 0, 128, False)
-    iota("xi", [[16, 128]], 0, 0, 0, 128)
-    if nq:
-        for b in range(2):
-            iota("wl%d" % b, [[V, nq], [0, CAP]], V * (r + 1), 0, V, V + CAP * nq)
 
     def ts(out, i, s1, s2, op0, op1, reads, writes, banks=(), q="V"):
         if op1 is None:
@@ -168,117 +188,128 @@ def rank_program(g, core, T, topo):
     def tt(out, i0, i1, o, reads, writes, banks=()):
         return op("V", lambda e: e.tensor_tensor(out, i0, i1, o), reads, writes, banks)
 
-    def cp(out, i, reads, writes, banks=()):
-        return op("V", lambda e: e.tensor_copy(out, i), reads, writes, banks)
+    def cp(out, i, reads, writes, banks=(), extra=()):
+        return op("V", lambda e: e.tensor_copy(out, i), reads, writes, banks, extra)
 
-    def R(name, lo=0, hi=1 << 20):
-        return (name, lo, min(hi, SCRATCH[name][1][-1]))
+    def act(out, i, f, reads, writes, banks=()):
+        return op("S", lambda e: e.activation(out, i, f), reads, writes, banks)
 
     def mset(ap, val, wr):
         op("V", lambda e: e.memset(ap, val), (), [wr])
 
-    ts(T.selx[:], T.iosx[:], T.iop[:], None, EQ, None, [R("iosx"), R("iop")], [R("selx")])
-    ts(T.idf[:], T.iom[:], T.iop[:], None, EQ, None, [R("iom"), R("iop")], [R("idf")])
-    cp(T.idb[:], T.idf[:], [R("idf")], [R("idb")])
-    ts(T.p16i[:], T.ip32[:], 112, None, AluOpType.bitwise_and, None, [R("ip32")], [R("p16i")])
-    ts(T.p15i[:], T.ip32[:], 15, None, AluOpType.bitwise_and, None, [R("ip32")], [R("p15i")])
-    cp(T.p16f[:], T.p16i[:], [R("p16i")], [R("p16f")])
-    cp(T.p15f[:], T.p15i[:], [R("p15i")], [R("p15f")])
+    iota("iop", [[1, 1]], 0, 1, 0, 1)
+    iota("ip32", [[1, 1]], 0, 1, 0, 1, False)
+    iota("iom", [[1, 128]], 0, 0, 0, 128)
     if nq:
-        ts(T.mm[:], T.im32[:], 112, None, AluOpType.bitwise_and, None, [R("im32")], [R("mm")])
-        ts(T.tg[:], T.iom[:], T.iop[:], None, GT, None, [R("iom"), R("iop")], [R("tg")])
-        ts(T.mg[:], T.mm[:], T.p16f[:], None, EQ, None, [R("mm"), R("p16f")], [R("mg")])
-        ts(T.id128[:], T.idf[:], 128.0, None, MUL, None, [R("idf")], [R("id128")])
-        tt(T.tg[:], T.tg[:], T.mg[:], MUL, [R("tg"), R("mg")], [R("tg")])
-        tt(T.id128[:], T.id128[:], T.tg[:], SUB, [R("id128"), R("tg")], [R("id128")])
-        cp(T.wa[:], T.id128[:], [R("id128")], [R("wa")])
-        tt(T.mg[:], T.mg[:], T.id128[:], ADD, [R("mg"), R("id128")], [R("mg")])
-        ts(T.wb[:], T.mg[:], -1.0, None, MUL, None, [R("mg")], [R("wb")])
-        ts(T.xi[:], T.xi[:], T.p15f[:], None, ADD, None, [R("xi"), R("p15f")], [R("xi")])
         mset(T.d0[:], 1.0, R("d0"))
         mset(T.oh0[:, 0:7 * SEG:SEG], 0.0, R("oh0"))
         mset(T.oh1[:, 0:7 * SEG:SEG], 0.0, R("oh1"))
         mset(T.d0[:, 0:7 * SEG:SEG], 0.0, R("d0"))
+        iota("im32", [[1, 128]], 0, 0, 0, 128, False)
+        iota("xi", [[16, 128]], 0, 0, 0, 128)
+    iota("iosx", [[1, 2], [16, 8]], 0, 0, 0, 16)
+    if nq:
+        for b in range(2):
+            iota("wl%d" % b, [[V, nq], [0, CAP]], V * (r + 1), 0, V, V + CAP * nq)
+    ts(T.p16i[:], T.ip32[:], 112, None, AluOpType.bitwise_and, None, [R("ip32")], [R("p16i")])
+    ts(T.p15i[:], T.ip32[:], 15, None, AluOpType.bitwise_and, None, [R("ip32")], [R("p15i")])
+    cp(T.p16f[:], T.p16i[:], [R("p16i")], [R("p16f")])
+    cp(T.p15f[:], T.p15i[:], [R("p15i")], [R("p15f")])
+    ts(T.idf[:], T.iom[:], T.iop[:], None, EQ, None, [R("iom"), R("iop")], [R("idf")])
+    if nq:
+        act(T.idb[:], T.idf[:], ACT.Copy, [R("idf")], [R("idb")])
+        ts(T.tg[:], T.iom[:], T.iop[:], None, GT, None, [R("iom"), R("iop")], [R("tg")])
+        ts(T.id128[:], T.idf[:], 128.0, None, MUL, None, [R("idf")], [R("id128")])
+        ts(T.mm[:], T.im32[:], 112, None, AluOpType.bitwise_and, None, [R("im32")], [R("mm")])
+        ts(T.mg[:], T.mm[:], T.p16f[:], None, EQ, None, [R("mm"), R("p16f")], [R("mg")])
+        tt(T.tg[:], T.tg[:], T.mg[:], MUL, [R("tg"), R("mg")], [R("tg")])
+        tt(T.id128[:], T.id128[:], T.tg[:], SUB, [R("id128"), R("tg")], [R("id128")])
+        act(T.wa[:], T.id128[:], ACT.Copy, [R("id128")], [R("wa")])
+        tt(T.mg[:], T.mg[:], T.id128[:], ADD, [R("mg"), R("id128")], [R("mg")])
+        ts(T.wb[:], T.mg[:], -1.0, None, MUL, None, [R("mg")], [R("wb")])
+    cp(T.rf[:], T.ri[:], [R("ri")], [R("rf")])
+    ts(T.rcol[:], T.rf[:], T.p16f[:], None, ADD, None, [R("rf"), R("p16f")], [R("rcol")])
+    for b in range(2):
+        lo, hi = 128 * b, 128 * b + 128
+        ts(T.roh[:, lo:hi], T.iom[:], T.rcol[:, b:b + 1], None, EQ, None, [R("iom"), R("rcol")], [R("roh", lo, hi)])
+    for b in range(2):
+        lo, hi = 128 * b, 128 * b + 128
+        op("T", lambda e: e.transpose(ps(7, lo, hi), T.roh[:, lo:hi], T.idf[:]), [R("roh", lo, hi), R("idf")], (), [7])
+    if nq:
+        act(T.srb[:], ps(7, 0, 256), ACT.Copy, (), [R("srb")], [7])
+    act(T.sr[:], ps(7, 0, 256), ACT.Copy, (), [R("sr")], [7])
+    if nq:
+        order("G", [R("srb")], (), (), ())
+        to_later(lambda k: T.srb[:], T.srl[:, 256 * r:256 * r + 256], "sra", "lss")
+        ts(T.xi[:], T.xi[:], T.p15f[:], None, ADD, None, [R("xi"), R("p15f")], [R("xi")])
     WC = BLK + BW * (9 - r)
-    for k in range(CHUNKS):
-        lo, hi = k * CW, (k + 1) * CW
-        cp(T.E0[:, lo:hi], T.ei[:, lo:hi], [R("ei", lo, hi)], [R("E0", lo, hi)])
+    iota("win", [[0, Z]], 0, 0, 0, Z)
+    if r == 0:
+        iota("win", [[0, 1]], 0, 0, Z, Z + 1)
+        iota("win", [[0, 1]], 0, 0, Z + V, Z + V + 1)
+    iota("win", [[0, WC - BLK]], 0, 0, BLK, WC)
+    ts(T.selx[:], T.iosx[:], T.iop[:], None, EQ, None, [R("iosx"), R("iop")], [R("selx")])
 
-    def late_constants():
-        for b in range(2):
-            w = "win%d" % b
-            mset(T[w][:, 0:LOC + 1], 0.0, R(w, 0, LOC + 1))
-            mset(T[w][:, BLK:WC], 0.0, R(w, BLK, WC))
-        cp(T.rf[:], T.ri[:], [R("ri")], [R("rf")])
-        ts(T.rcol[:], T.rf[:], T.p16f[:], None, ADD, None, [R("rf"), R("p16f")], [R("rcol")])
-        for b in range(2):
-            ts(T.roh[:, 128 * b:128 * b + 128], T.iom[:], T.rcol[:, b:b + 1], None, EQ, None, [R("iom"), R("rcol")], [R("roh", 128 * b, 128 * b + 128)])
+    def convert():
+        for k in range(CHUNKS):
+            lo, hi = k * CW, (k + 1) * CW
+            cp(T.E0[:, lo:hi], T.ei[:, lo:hi], [R("ei", lo, hi)], [R("E0", lo, hi)])
 
     for n in range(RO):
         E, X = ("E0", "E1") if n % 2 == 0 else ("E1", "E0")
-        for i in range(16):
-            op("T", lambda e: e.matmul(T.ps0[:, i:256:16], T[E][:, i:V:16], T.selx[:], True, True), [R(E), R("selx")], (), [0])
-        ts(T.xs[:], ps(0, 0, 256), -1023.75, None, ADD, None, (), [R("xs")], [0])
+        tw = (1, 0)
+        if n:
+            for i in range(16):
+                op("T", lambda e: e.matmul(T.ps0[:, i:256:16], T[E][:, i:V:16], T.selx[:], True, True), [R(E), R("selx")], (), [0])
         for b in range(2):
-            op("T", lambda e: e.transpose(ps(1, 128 * b, 128 * b + 128), T.xs[:, 128 * b:128 * b + 128], T.idf[:]), [R("xs"), R("idf")], (), [1])
-        ts(T.qb[:], ps(1, 0, 256), ROUND_C, ROUND_C, ADD, SUB, (), [R("qb")], [1])
+            lo, hi = 128 * b, 128 * b + 128
+            if n:
+                ts(T.xs[:, lo:hi], ps(0, lo, hi), -1023.75, None, ADD, None, (), [R("xs", lo, hi)], [0])
+            else:
+                ts(T.xs[:, lo:hi], T.xw[:, lo:hi], -1023.75, None, ADD, None, [R("xw", lo, hi)], [R("xs", lo, hi)])
+        for b in range(2):
+            lo, hi = 128 * b, 128 * b + 128
+            op("T", lambda e: e.transpose(ps(tw[b], 256, 384), T.xs[:, lo:hi], T.idf[:]), [R("xs", lo, hi), R("idf")], (), [tw[b]])
+        for b in range(2):
+            lo, hi = 128 * b, 128 * b + 128
+            ts(T.qb[:, lo:hi], ps(tw[b], 256, 384), ROUND_C, ROUND_C, ADD, SUB, (), [R("qb", lo, hi)], [tw[b]])
         if nq:
             na = min(4, nq)
             for b in range(2):
                 oh, sc = "oh%d" % b, "sc%d" % b
                 for k, q in enumerate(later):
                     ts(T[oh][:, k * SEG + 1:(k + 1) * SEG], T.qb[:, 128 * b:128 * b + 128], float(V * q), None, EQ, None,
-                       [R("qb")], [R(oh, k * SEG + 1, (k + 1) * SEG)])
+                       [R("qb", 128 * b, 128 * b + 128)], [R(oh, k * SEG + 1, (k + 1) * SEG)])
                 op("V", lambda e: e.tensor_tensor_scan(T[sc][:, 0:nq * SEG], T.d0[:, 0:nq * SEG], T[oh][:, 0:nq * SEG], 0.0, MUL, ADD),
                    [R(oh), R("d0")], [R(sc)])
             ts(T.rqv[:], T.qb[:], 1.0 / 16, float(V - 1 - CAP * (r + 1)), MUL, ADD, [R("qb")], [R("rqv")])
-
-            def count(b, part):
-                sc, bk = "sc%d" % b, 2 + 2 * b + part
-                for k in (range(na) if part == 0 else range(na, nq)):
-                    lo = (k % 4) * CAP
+            for b in range(2):
+                sc = "sc%d" % b
+                for k in range(nq):
+                    bk, lo = 2 + 2 * b + k // 4, (k % 4) * CAP
                     op("T", lambda e: e.matmul(ps(bk, lo, lo + CAP), T.wa[:], T[sc][:, k * SEG + 1:(k + 1) * SEG], True, False), [R(sc), R("wa")], (), [bk])
                     op("T", lambda e: e.matmul(ps(bk, lo, lo + CAP), T.wb[:], T[sc][:, k * SEG:(k + 1) * SEG - 1], False, True), [R(sc), R("wb")], (), [bk])
-
-            def positive(b, part):
-                rl, bk = "rl%d" % b, 2 + 2 * b + part
-                lo, hi = (0, na * CAP) if part == 0 else (na * CAP, nq * CAP)
-                if hi == lo:
-                    return
-                if part == 0:
-                    op("S", lambda e: e.activation(T[rl][:, lo:hi], ps(bk, 0, hi - lo), ACT.Relu), (), [R(rl, lo, hi)], [bk])
-                else:
-                    ts(T[rl][:, lo:hi], ps(bk, 0, hi - lo), 0.0, None, MAX, None, (), [R(rl, lo, hi)], [bk])
-
-            def slots(b):
+            for b in range(2):
+                for lo, hi, bk in ((0, na * CAP, 2 + 2 * b), (na * CAP, nq * CAP, 3 + 2 * b)):
+                    if hi > lo:
+                        act(T["rl%d" % b][:, lo:hi], ps(bk, 0, hi - lo), ACT.Relu, (), [R("rl%d" % b, lo, hi)], [bk])
+            for b in range(2):
                 rl = "rl%d" % b
                 for k in range(nq):
                     op("T", lambda e: e.matmul(ps(6 + b, 0, CAP), T.idb[:], T[rl][:, k * CAP:(k + 1) * CAP], k == 0, k == nq - 1),
                        [R(rl, k * CAP, (k + 1) * CAP), R("idb")], (), [6 + b])
-
-            def places(b):
-                lo, hi = 128 * b, 128 * b + 128
-                ts(T.yv[:, lo:hi], ps(6 + b, 0, CAP), 4096.0, -1.0, MUL, ADD, (), [R("yv", lo, hi)], [6 + b])
-                tt(T.zv[:, lo:hi], ps(6 + b, 0, CAP), T.rqv[:, lo:hi], ADD, [R("rqv")], [R("zv", lo, hi)], [6 + b])
-                tt(T.zv[:, lo:hi], T.zv[:, lo:hi], T.yv[:, lo:hi], MIN, [R("zv", lo, hi), R("yv", lo, hi)], [R("zv", lo, hi)])
-                tt(T.zv[:, lo:hi], T.zv[:, lo:hi], T.xi[:], MAX, [R("zv", lo, hi), R("xi")], [R("zv", lo, hi)])
+            if n == 0:
+                convert()
+            for b in range(2):
+                lo, hi, zb = 128 * b, 128 * b + 128, 2 + 2 * b
+                ts(T.yv[:, lo:hi], ps(6 + b, 0, CAP), 4096.0, -float(Z), MUL, ADD, (), [R("yv", lo, hi)], [6 + b])
+                tt(ps(zb, 0, CAP), ps(6 + b, 0, CAP), T.rqv[:, lo:hi], ADD, [R("rqv")], [R("ps%d" % zb)], [6 + b, zb])
+                tt(ps(zb, 0, CAP), ps(zb, 0, CAP), T.yv[:, lo:hi], MIN, [R("yv", lo, hi), R("ps%d" % zb)], [R("ps%d" % zb)], [zb])
+                tt(T.zv[:, lo:hi], ps(zb, 0, CAP), T.xi[:], MAX, [R("xi"), R("ps%d" % zb)], [R("zv", lo, hi)], [zb])
                 cp(T.o16[:, lo:hi], T.zv[:, lo:hi], [R("zv", lo, hi)], [R("o16", lo, hi)])
-
             LH = V + CAP * nq
-            count(0, 0)
-            count(0, 1)
-            positive(0, 0)
-            positive(0, 1)
-            count(1, 0)
-            positive(1, 0)
-            slots(0)
-            count(1, 1)
-            places(0)
-            op("S", lambda e: e.activation(T.wl0[:, 0:LH].indirect(T.o16[:, 0:128]), T[E][:], ACT.Silu), [R(E), R("o16", 0, 128)], [R("wl0", 0, LH)])
-            positive(1, 1)
-            slots(1)
-            places(1)
-            op("V", lambda e: e.tensor_copy(T.wl1[:, 0:LH].indirect(T.o16[:, 128:256]), T[E][:]), [R(E), R("o16", 128, 256)], [R("wl1", 0, LH)])
+            act(T.wl0[:, 0:LH].indirect(T.o16[:, 0:128]), T[E][:], ACT.Silu, [R(E), R("o16", 0, 128)], [R("wl0", 0, LH)])
+            cp(T.wl1[:, 0:LH].indirect(T.o16[:, 128:256]), T[E][:], [R(E), R("o16", 128, 256)], [R("wl1", 0, LH)])
             before = [("lsq", total["lsq"])] if n else []
             for b in range(2):
                 wl, items = "wl%d" % b, []
@@ -287,80 +318,76 @@ def rank_program(g, core, T, topo):
                     items.append((T.rqb[k, b::2, :], T[wl][b::16, lo:lo + CAP], [R(wl, lo, lo + CAP)], ()))
                 tok = dmas("S" if b == 0 else "Y", "dq%d" % b, items, before)
                 need("G", tok[0], tok[1])
-            outs = [c for c in (cores[q] for q in later) if c in far]
-            w = 1
-            while 2 * w * max(len(later), 1) <= len(pool):
-                w *= 2
-            transfers = []
-            for k, q in enumerate(later):
-                rid, pid, _s = topo.addr(cores[q])
-                transfers.append(RemoteDMATransfer(dst_ids=[DstId(rid=rid, pnc=pid)], dma_engine_mask=rem_mask(pool[k * w:(k + 1) * w]),
-                                                   remote_sem=T.sem["rq%d" % r], src=T.rqb[k], dst=T.rland[r], alu_op=0))
-            g.remote_dma_fused(transfers, local_sem=T.sem.lsq)
-            tokens("lsq", w * nq)
-        if n == 0:
-            late_constants()
-            for b in range(2):
-                op("T", lambda e: e.transpose(ps(0, 128 * b, 128 * b + 128), T.roh[:, 128 * b:128 * b + 128], T.idf[:]),
-                   [R("roh", 128 * b, 128 * b + 128), R("idf")], (), [0])
-            cp(T.sr[:], ps(0, 0, 256), (), [R("sr")], [0])
+            to_later(lambda k: T.rqb[k], T.rland[r], "rq%d" % r, "lsq")
+        elif n == 0:
+            convert()
         for b in range(2):
-            w = "win%d" % b
             for k in range(4):
                 bk, lo = 2 + k, 512 * k
                 op("T", lambda e: e.matmul(ps(bk, 0, 512), T.sr[:, 128 * b:128 * b + 128], T[E][:, lo:lo + 512], True, True), [R("sr"), R(E, lo, lo + 512)], (), [bk])
                 s = 1 if (k == 0 and r == 0) else 0
-                op("S", lambda e: e.activation(T[w][:, LOC + lo + s:LOC + lo + 512], ps(bk, s, 512), ACT.Copy), (), [R(w, LOC + lo + s, LOC + lo + 512)], [bk])
-        ts(T.u1[:], T.qb[:], 8.0, 1023.75 - V * r - 8.0 * V * r + LOC + 1, MUL, ADD, [R("qb")], [R("u1")])
-        ts(T.a1[:], T.qb[:], 17.0 / 256, float(BLK + 1 - BW * r), MUL, ADD, [R("qb")], [R("a1")])
-        tt(T.u1[:], ps(1, 0, 256), T.u1[:], ADD, [R("u1")], [R("u1")], [1])
+                c0 = Z + V * b + lo
+                act(T.win[:, c0 + s:c0 + 512], ps(bk, s, 512), ACT.Copy, (), [R("win", c0 + s, c0 + 512)], [bk])
+        for b in range(2):
+            lo, hi = 128 * b, 128 * b + 128
+            ts(T.u1[:, lo:hi], T.qb[:, lo:hi], 8.0, 1023.75 - V * r - 8.0 * V * r + Z + V * b + Z, MUL, ADD, [R("qb", lo, hi)], [R("u1", lo, hi)])
+            ts(T.a1[:, lo:hi], T.qb[:, lo:hi], BW / 2048.0, float(BLK + Z + b - BW * r), MUL, ADD, [R("qb", lo, hi)], [R("a1", lo, hi)])
+            tt(T.u1[:, lo:hi], ps(tw[b], 256, 384), T.u1[:, lo:hi], ADD, [R("u1", lo, hi)], [R("u1", lo, hi)], [tw[b]])
         tt(T.u1[:], T.u1[:], T.a1[:], MIN, [R("u1"), R("a1")], [R("u1")])
         if nq:
             for b in range(2):
                 lo, hi = 128 * b, 128 * b + 128
                 ts(T.si[:, lo:hi], ps(6 + b, 0, CAP), -1.0, 129.0, ADD, MUL, (), [R("si", lo, hi)], [6 + b])
-            ts(T.si[:], T.si[:], 4, 127, AluOpType.arith_shift_right, AluOpType.bitwise_and, [R("si")], [R("si")])
+            ts(T.si[:], T.si[:], 3, 254, AluOpType.arith_shift_right, AluOpType.bitwise_and, [R("si")], [R("si")])
             tt(T.av[:], T.yv[:], T.si[:], MIN, [R("yv"), R("si")], [R("av")])
             tt(T.av[:], T.av[:], T.u1[:], ADD, [R("av"), R("u1")], [R("av")])
         else:
-            ts(T.av[:], T.u1[:], -1.0, None, ADD, None, [R("u1")], [R("av")])
+            ts(T.av[:], T.u1[:], -float(Z), None, ADD, None, [R("u1")], [R("av")])
         cp(T.a16[:], T.av[:], [R("av")], [R("a16")])
-        for p in range(nr):
-            w = 1
-            while 2 * w * max(N - 1 - p, 1) <= 8:
-                w *= 2
-            arr = tokens("rq%d" % p, w)
-            c0 = 16 * p
-            dmas("Y", "lw%d" % p, [(T.lq[:, c0:c0 + 16], T.rland[p], (), [R("lq", c0, c0 + 16)])], [arr])
-            ts(T.lo[:, c0:c0 + 16], T.lq[:, c0:c0 + 16], 0.25 - V * r, None, ADD, None, [R("lq", c0, c0 + 16)], [R("lo", c0, c0 + 16)])
+        if n == 0 and nr:
+            got = tokens("sra", sum(width(topo, cores, p) for p in range(nr)))
+            cp(T.srf[:, 0:256 * nr], T.srl[:, 0:256 * nr], (), [R("srf", 0, 256 * nr)], (), [got])
+
+        def gather(p):
+            c0, c1 = 16 * p, 16 * p + 16
+            arr = tokens("rq%d" % p, width(topo, cores, p))
+            dmas("Y", "lw%d" % p, [(T.lq[:, c0:c1], T.rland[p], (), [R("lq", c0, c1)])], [arr])
+            ts(T.lo[:, c0:c1], T.lq[:, c0:c1], 0.25 - V * r, None, ADD, None, [R("lq", c0, c1)], [R("lo", c0, c1)])
+            cp(T.rpf[:, 16 * c0:16 * c1], T[E][:, 0:V].indirect(T.lo[:, c0:c1]), [R(E), R("lo", c0, c1)], [R("rpf", 16 * c0, 16 * c1)])
+            bk = (0, 1, 6, 7)[p % 4]
+            for b in range(2):
+                m = 256 * p + 128 * b
+                op("T", lambda e: e.matmul(T["ps%d" % bk][:, b:256:2], T.srf[:, m:m + 128], T.rpf[:, 256 * p + b:256 * p + 256:2], True, True),
+                   [R("srf", m, m + 128), R("rpf", 16 * c0, 16 * c1)], (), [bk])
+
+        def reply(p):
+            lo, hi, bk = 256 * p, 256 * p + 256, (0, 1, 6, 7)[p % 4]
             left = [("ls%d" % p, total["ls%d" % p])] if n else []
-            tok = op("V", lambda e: e.tensor_copy(T.rp[:, 256 * p:256 * p + 256], T[E][:, 0:V].indirect(T.lo[:, c0:c0 + 16])),
-                     [R(E), R("lo", c0, c0 + 16)], [R("rp", 256 * p, 256 * p + 256)], (), left)
+            tok = cp(T.rp[:, lo:hi], ps(bk, 0, 256), (), [R("rp", lo, hi)], [bk], left)
             need("G", tok[0], tok[1])
             rid, pid, _s = topo.addr(cores[p])
             k = r - p - 1
-            g.remote_dma(out_ap=T.ld[:, 256 * k:256 * k + 256], in_ap=T.rp[:, 256 * p:256 * p + 256], remote_sem=T.sem["rp%d" % r],
+            g.remote_dma(out_ap=T.ld[:, 256 * k:256 * k + 256], in_ap=T.rp[:, lo:hi], remote_sem=T.sem["rp%d" % r],
                          local_sem=T.sem["ls%d" % p], pid=pid, routing_id=rid, dma_engine_mask=rem_mask(pool))
             tokens("ls%d" % p, len(pool))
+        if nr:
+            gather(0)
+            reply(0)
+        for p in range(1, nr + 1):
+            if p < nr:
+                gather(p)
+            if p > 1:
+                reply(p - 1)
         for k, q in enumerate(later):
-            arr = tokens("rp%d" % q, len(pool))
-            lo = 256 * k
-            op("V", lambda e: e.tensor_copy(T.ldf[:, lo:lo + 256], T.ld[:, lo:lo + 256]), (), [R("ldf", lo, lo + 256)], (), [arr])
-            bk = (0, 1, 6, 7)[k % 4]
-            for b in range(2):
-                op("T", lambda e: e.matmul(ps(bk, 128 * b, 128 * b + 128), T.sr[:, 128 * b:128 * b + 128], T.ldf[:, lo + b:lo + 256:2], True, True),
-                   [R("ldf", lo, lo + 256), R("sr")], (), [bk])
-            c0 = BLK + BW * (k + 1) + 1
-            for b in range(2):
-                w = "win%d" % b
-                op("S", lambda e: e.activation(T[w][:, c0:c0 + CAP], ps(bk, 128 * b, 128 * b + 128), ACT.Copy), (), [R(w, c0, c0 + CAP)], [bk])
-        op("V", lambda e: e.tensor_tensor(T[X][:], T.win0[:, 0:WC].indirect(T.a16[:, 0:128]), T[E][:], MAX),
-           [R("win0", 0, WC), R("a16"), R(E)], [R(X)])
-        pieces = 1 if n < RO - 1 else 4
+            arr = tokens("rp%d" % q, len(out_engines(topo, cores, q)))
+            c0 = BLK + BW * (k + 1) + Z
+            cp(T.win[:, c0:c0 + 256], T.ld[:, 256 * k:256 * k + 256], (), [R("win", c0, c0 + 256)], (), [arr])
+        op("V", lambda e: e.tensor_tensor(T[X][:], T.win[:, 0:WC].indirect(T.a16[:, 0:128]), T[E][:], MAX), [R("win", 0, WC), R("a16"), R(E)], [R(X)])
+        pieces = 1 if n < RO - 1 else PIECES
         for k in range(pieces):
             lo, hi = k * V // pieces, (k + 1) * V // pieces
-            op("V", lambda e: e.tensor_tensor(T[X][:, lo:hi], T.win1[:, 0:WC].indirect(T.a16[:, 128 + lo // 16:128 + hi // 16]), T[X][:, lo:hi], MAX),
-               [R("win1", 0, WC), R("a16"), R(X, lo, hi)], [R(X, lo, hi)])
+            op("V", lambda e: e.tensor_tensor(T[X][:, lo:hi], T.win[:, 0:WC].indirect(T.a16[:, 128 + lo // 16:128 + hi // 16]), T[X][:, lo:hi], MAX),
+               [R("win", 0, WC), R("a16"), R(X, lo, hi)], [R(X, lo, hi)])
             if n == RO - 1:
                 dmas("Y" if k % 2 == 0 else "S", "st%d" % k, [(T.y[:, lo:hi], T[X][:, lo:hi], [R(X, lo, hi)], ())])
     for sem in sorted(total):

import numpy as np
from concourse.bass import DstId, RemoteDMATransfer
from concourse.mybir import AluOpType, ActivationFunctionType

V, N, RO, CAP = 2048, 8, 3, 128
SEG = CAP + 1
Z = 8
BLK = Z + 2 * V
BW = Z + 2 * CAP
WCOLS = BLK + 9 * BW
LCOLS = V + 7 * CAP
CHUNKS, PIECES = 4, 8
ROUND_C = 1.5 * 2.0 ** 34

SCRATCH = {
    "ei": ("sbuf", [128, V], "int32"), "E0": ("sbuf", [128, V], "float32"), "E1": ("sbuf", [128, V], "float32"),
    "xw": ("sbuf", [128, 256], "int32"), "win": ("sbuf", [128, WCOLS], "float32"),
    "wl0": ("sbuf", [128, LCOLS], "float32"), "wl1": ("sbuf", [128, LCOLS], "float32"),
    "ri": ("sbuf", [128, 2], "int32"), "rf": ("sbuf", [128, 2], "float32"), "rcol": ("sbuf", [128, 2], "float32"),
    "iom": ("sbuf", [128, 128], "float32"), "iop": ("sbuf", [128, 1], "float32"), "iosx": ("sbuf", [128, 16], "float32"),
    "ip32": ("sbuf", [128, 1], "int32"), "im32": ("sbuf", [128, 128], "int32"),
    "p16i": ("sbuf", [128, 1], "int32"), "p15i": ("sbuf", [128, 1], "int32"),
    "p16f": ("sbuf", [128, 1], "float32"), "p15f": ("sbuf", [128, 1], "float32"),
    "mm": ("sbuf", [128, 128], "int32"), "mg": ("sbuf", [128, 128], "float32"), "tg": ("sbuf", [128, 128], "float32"),
    "idf": ("sbuf", [128, 128], "float32"), "id128": ("sbuf", [128, 128], "float32"), "selx": ("sbuf", [128, 16], "float32"),
    "idb": ("sbuf", [128, 128], "bfloat16"), "wa": ("sbuf", [128, 128], "bfloat16"), "wb": ("sbuf", [128, 128], "bfloat16"),
    "xi": ("sbuf", [128, 128], "float32"), "d0": ("sbuf", [128, 7 * SEG], "bfloat16"),
    "oh0": ("sbuf", [128, 7 * SEG], "bfloat16"), "oh1": ("sbuf", [128, 7 * SEG], "bfloat16"),
    "sc0": ("sbuf", [128, 7 * SEG], "bfloat16"), "sc1": ("sbuf", [128, 7 * SEG], "bfloat16"),
    "rl0": ("sbuf", [128, 7 * CAP], "bfloat16"), "rl1": ("sbuf", [128, 7 * CAP], "bfloat16"),
    "roh": ("sbuf", [128, 256], "float32"), "sr": ("sbuf", [128, 256], "float32"), "srb": ("sbuf", [128, 256], "bfloat16"),
    "srl": ("sbuf", [128, 7 * 256], "bfloat16"), "srf": ("sbuf", [128, 7 * 256], "float32"),
    "xs": ("sbuf", [128, 256], "float32"), "qb": ("sbuf", [128, 256], "bfloat16"), "rqv": ("sbuf", [128, 256], "float32"),
    "yv": ("sbuf", [128, 256], "float32"), "zv": ("sbuf", [128, 256], "float32"), "o16": ("sbuf", [128, 256], "uint16"),
    "u1": ("sbuf", [128, 256], "float32"), "a1": ("sbuf", [128, 256], "float32"),
    "si": ("sbuf", [128, 256], "int32"), "av": ("sbuf", [128, 256], "float32"), "a16": ("sbuf", [128, 256], "uint16"),
    "lq": ("sbuf", [128, 7 * 16], "float32"), "lo": ("sbuf", [128, 7 * 16], "uint16"), "rpf": ("sbuf", [128, 7 * 256], "float32"),
    "rp": ("sbuf", [128, 7 * 256], "uint16"), "ld": ("sbuf", [128, 7 * 256], "uint16"),
    "rqb": ("dram", [7, 128, 16], "float32"), "rland": ("dram", [7, 128, 16], "float32"),
}
for _k in range(8):
    SCRATCH["ps%d" % _k] = ("psum", [128, 512], "float32")
SEMAPHORES = (["qV", "qT", "qS", "qG", "lri", "lx0", "lx1", "dq0", "dq1", "lsq", "lss", "sra"]
              + ["le%d" % k for k in range(CHUNKS)] + ["st%d" % k for k in range(PIECES)]
              + ["rq%d" % k for k in range(7)] + ["rp%d" % k for k in range(8)] + ["ls%d" % k for k in range(7)] + ["lw%d" % k for k in range(7)])

ADD, SUB, MUL, MAX, MIN, EQ, GT = (AluOpType.add, AluOpType.subtract, AluOpType.mult, AluOpType.max, AluOpType.min,
                                   AluOpType.is_equal, AluOpType.is_gt)
ACT = ActivationFunctionType


def out_engines(topo, cores, q):
    far = [c for c in cores if topo.chip(c) != topo.chip(cores[q])]
    return topo.engines(cores[q], far[0])


def width(topo, cores, p):
    n, w = len(out_engines(topo, cores, p)), 1
    while 2 * w * max(N - 1 - p, 1) <= n:
        w *= 2
    return w


def rank_program(g, core, T, topo):
    r = T.rank_of(core)
    if r is None:
        return
    cores = T.cores
    later = list(range(r + 1, N))
    nq, nr = len(later), r
    Q = {"V": g.vector, "T": g.tensor, "S": g.scalar, "Y": g.sync, "G": g}
    total, clock, snap, acc, bank = {}, {q: {} for q in Q}, {}, {}, {}

    def need(q, sem, val):
        ck = clock[q]
        if ck.get(sem, 0) >= val:
            return
        Q[q].wait_ge(T.sem[sem], val)
        ck[sem] = val
        for k, v in snap.get((sem, val), {}).items():
            if ck.get(k, 0) < v:
                ck[k] = v

    def order(q, reads, writes, banks, extra):
        want = {}

        def add(tok):
            if want.get(tok[0], 0) < tok[1]:
                want[tok[0]] = tok[1]
        for (b, lo, hi) in reads:
            for e in acc.get(b, []):
                if e[4] and e[0] < hi and lo < e[1]:
                    add(e[2])
        for (b, lo, hi) in writes:
            for e in acc.get(b, []):
                if e[0] < hi and lo < e[1]:
                    add(e[2])
        for k in banks:
            for oq, tok in bank.get(k, {}).items():
                if oq != q:
                    add(tok)
        for tok in extra:
            add(tok)
        for sem in sorted(want, key=lambda s: (s[0] != "q", s)):
            need(q, sem, want[sem])

    def note(q, tok, reads, writes, banks):
        s = dict(clock[q])
        s[tok[0]] = tok[1]
        snap[tok] = s
        for (b, lo, hi) in writes:
            keep = [e for e in acc.get(b, []) if not (lo <= e[0] and e[1] <= hi)]
            keep.append((lo, hi, tok, q, True))
            acc[b] = keep
        for (b, lo, hi) in reads:
            keep = [e for e in acc.get(b, []) if e[4] or e[3] != q or (e[0], e[1]) != (lo, hi) or e[2][0] != tok[0]]
            keep.append((lo, hi, tok, q, False))
            acc[b] = keep
        for k in banks:
            bank.setdefault(k, {})[q] = tok

    def op(q, fn, reads=(), writes=(), banks=(), extra=()):
        order(q, reads, writes, banks, extra)
        sem = "q" + q
        total[sem] = total.get(sem, 0) + 1
        fn(Q[q]).then_inc(T.sem[sem], 1)
        note(q, (sem, total[sem]), reads, writes, banks)
        return (sem, total[sem])

    def dmas(q, sem, items, extra=()):
        tok = (sem, total.get(sem, 0) + 16 * len(items))
        total[sem] = tok[1]
        for (o, i, rd, wr) in items:
            order(q, rd, wr, (), extra)
            Q[q].dma_start(o, i).then_inc(T.sem[sem], 16)
        for (o, i, rd, wr) in items:
            note(q, tok, rd, wr, ())
        return tok

    def tokens(sem, n):
        total[sem] = total.get(sem, 0) + n
        return (sem, total[sem])

    def ps(k, lo, hi):
        return T["ps%d" % k][:, lo:hi]

    def rem_mask(engs):
        m = 0
        for e in engs:
            m |= 1 << e
        return m

    def R(name, lo=0, hi=1 << 20):
        return (name, lo, min(hi, SCRATCH[name][1][-1]))

    pool = out_engines(topo, cores, r)

    def to_later(src, dst, remote, local):
        w, transfers = width(topo, cores, r), []
        for k, q in enumerate(later):
            rid, pid, _s = topo.addr(cores[q])
            transfers.append(RemoteDMATransfer(dst_ids=[DstId(rid=rid, pnc=pid)], dma_engine_mask=rem_mask(pool[k * w:(k + 1) * w]),
                                               remote_sem=T.sem[remote], src=src(k), dst=dst, alu_op=0))
        g.remote_dma_fused(transfers, local_sem=T.sem[local])
        tokens(local, w * nq)

    CW = V // CHUNKS
    dmas("S", "lri", [(T.ri[:], T.rights[:], (), [R("ri")])])
    for b in range(2):
        dmas("Y" if b == 0 else "S", "lx%d" % b,
             [(T.xw[:, 128 * b + 16 * s:128 * b + 16 * s + 16], T.ends[16 * s + b:16 * s + b + 1, :], (),
               [R("xw", 128 * b + 16 * s, 128 * b + 16 * s + 16)]) for s in range(8)])
    for k in range(CHUNKS):
        lo, hi = k * CW, (k + 1) * CW
        dmas("Y" if k % 2 == 0 else "S", "le%d" % k, [(T.ei[:, lo:hi], T.ends[:, lo:hi], (), [R("ei", lo, hi)])])

    def iota(name, pat, base, cm, lo, hi, f32=True):
        if f32:
            op("G", lambda e: e.iota(T[name][:, lo:hi], pat, base, cm, allow_small_or_imprecise_dtypes=True), (), [(name, lo, hi)])
        else:
            op("G", lambda e: e.iota(T[name][:, lo:hi], pat, base, cm), (), [(name, lo, hi)])

    def ts(out, i, s1, s2, op0, op1, reads, writes, banks=(), q="V"):
        if op1 is None:
            return op(q, lambda e: e.tensor_scalar(out, i, s1, None, op0), reads, writes, banks)
        return op(q, lambda e: e.tensor_scalar(out, i, s1, s2, op0, op1), reads, writes, banks)

    def tt(out, i0, i1, o, reads, writes, banks=()):
        return op("V", lambda e: e.tensor_tensor(out, i0, i1, o), reads, writes, banks)

    def cp(out, i, reads, writes, banks=(), extra=()):
        return op("V", lambda e: e.tensor_copy(out, i), reads, writes, banks, extra)

    def act(out, i, f, reads, writes, banks=()):
        return op("S", lambda e: e.activation(out, i, f), reads, writes, banks)

    def mset(ap, val, wr):
        op("V", lambda e: e.memset(ap, val), (), [wr])

    iota("iop", [[1, 1]], 0, 1, 0, 1)
    iota("ip32", [[1, 1]], 0, 1, 0, 1, False)
    iota("iom", [[1, 128]], 0, 0, 0, 128)
    if nq:
        mset(T.d0[:], 1.0, R("d0"))
        mset(T.oh0[:, 0:7 * SEG:SEG], 0.0, R("oh0"))
        mset(T.oh1[:, 0:7 * SEG:SEG], 0.0, R("oh1"))
        mset(T.d0[:, 0:7 * SEG:SEG], 0.0, R("d0"))
        iota("im32", [[1, 128]], 0, 0, 0, 128, False)
        iota("xi", [[16, 128]], 0, 0, 0, 128)
    iota("iosx", [[1, 2], [16, 8]], 0, 0, 0, 16)
    if nq:
        for b in range(2):
            iota("wl%d" % b, [[V, nq], [0, CAP]], V * (r + 1), 0, V, V + CAP * nq)
    ts(T.p16i[:], T.ip32[:], 112, None, AluOpType.bitwise_and, None, [R("ip32")], [R("p16i")])
    ts(T.p15i[:], T.ip32[:], 15, None, AluOpType.bitwise_and, None, [R("ip32")], [R("p15i")])
    cp(T.p16f[:], T.p16i[:], [R("p16i")], [R("p16f")])
    cp(T.p15f[:], T.p15i[:], [R("p15i")], [R("p15f")])
    ts(T.idf[:], T.iom[:], T.iop[:], None, EQ, None, [R("iom"), R("iop")], [R("idf")])
    if nq:
        act(T.idb[:], T.idf[:], ACT.Copy, [R("idf")], [R("idb")])
        ts(T.tg[:], T.iom[:], T.iop[:], None, GT, None, [R("iom"), R("iop")], [R("tg")])
        ts(T.id128[:], T.idf[:], 128.0, None, MUL, None, [R("idf")], [R("id128")])
        ts(T.mm[:], T.im32[:], 112, None, AluOpType.bitwise_and, None, [R("im32")], [R("mm")])
        ts(T.mg[:], T.mm[:], T.p16f[:], None, EQ, None, [R("mm"), R("p16f")], [R("mg")])
        tt(T.tg[:], T.tg[:], T.mg[:], MUL, [R("tg"), R("mg")], [R("tg")])
        tt(T.id128[:], T.id128[:], T.tg[:], SUB, [R("id128"), R("tg")], [R("id128")])
        act(T.wa[:], T.id128[:], ACT.Copy, [R("id128")], [R("wa")])
        tt(T.mg[:], T.mg[:], T.id128[:], ADD, [R("mg"), R("id128")], [R("mg")])
        ts(T.wb[:], T.mg[:], -1.0, None, MUL, None, [R("mg")], [R("wb")])
    cp(T.rf[:], T.ri[:], [R("ri")], [R("rf")])
    ts(T.rcol[:], T.rf[:], T.p16f[:], None, ADD, None, [R("rf"), R("p16f")], [R("rcol")])
    for b in range(2):
        lo, hi = 128 * b, 128 * b + 128
        ts(T.roh[:, lo:hi], T.iom[:], T.rcol[:, b:b + 1], None, EQ, None, [R("iom"), R("rcol")], [R("roh", lo, hi)])
    for b in range(2):
        lo, hi = 128 * b, 128 * b + 128
        op("T", lambda e: e.transpose(ps(7, lo, hi), T.roh[:, lo:hi], T.idf[:]), [R("roh", lo, hi), R("idf")], (), [7])
    if nq:
        act(T.srb[:], ps(7, 0, 256), ACT.Copy, (), [R("srb")], [7])
    act(T.sr[:], ps(7, 0, 256), ACT.Copy, (), [R("sr")], [7])
    if nq:
        order("G", [R("srb")], (), (), ())
        to_later(lambda k: T.srb[:], T.srl[:, 256 * r:256 * r + 256], "sra", "lss")
        ts(T.xi[:], T.xi[:], T.p15f[:], None, ADD, None, [R("xi"), R("p15f")], [R("xi")])
    WC = BLK + BW * (9 - r)
    iota("win", [[0, Z]], 0, 0, 0, Z)
    if r == 0:
        iota("win", [[0, 1]], 0, 0, Z, Z + 1)
        iota("win", [[0, 1]], 0, 0, Z + V, Z + V + 1)
    iota("win", [[0, WC - BLK]], 0, 0, BLK, WC)
    ts(T.selx[:], T.iosx[:], T.iop[:], None, EQ, None, [R("iosx"), R("iop")], [R("selx")])

    def convert():
        for k in range(CHUNKS):
            lo, hi = k * CW, (k + 1) * CW
            cp(T.E0[:, lo:hi], T.ei[:, lo:hi], [R("ei", lo, hi)], [R("E0", lo, hi)])

    for n in range(RO):
        E, X = ("E0", "E1") if n % 2 == 0 else ("E1", "E0")
        tw = (1, 0)
        if n:
            for i in range(16):
                op("T", lambda e: e.matmul(T.ps0[:, i:256:16], T[E][:, i:V:16], T.selx[:], True, True), [R(E), R("selx")], (), [0])
        for b in range(2):
            lo, hi = 128 * b, 128 * b + 128
            if n:
                ts(T.xs[:, lo:hi], ps(0, lo, hi), -1023.75, None, ADD, None, (), [R("xs", lo, hi)], [0])
            else:
                ts(T.xs[:, lo:hi], T.xw[:, lo:hi], -1023.75, None, ADD, None, [R("xw", lo, hi)], [R("xs", lo, hi)])
        for b in range(2):
            lo, hi = 128 * b, 128 * b + 128
            op("T", lambda e: e.transpose(ps(tw[b], 256, 384), T.xs[:, lo:hi], T.idf[:]), [R("xs", lo, hi), R("idf")], (), [tw[b]])
        for b in range(2):
            lo, hi = 128 * b, 128 * b + 128
            ts(T.qb[:, lo:hi], ps(tw[b], 256, 384), ROUND_C, ROUND_C, ADD, SUB, (), [R("qb", lo, hi)], [tw[b]])
        if nq:
            na = min(4, nq)
            for b in range(2):
                oh, sc = "oh%d" % b, "sc%d" % b
                for k, q in enumerate(later):
                    ts(T[oh][:, k * SEG + 1:(k + 1) * SEG], T.qb[:, 128 * b:128 * b + 128], float(V * q), None, EQ, None,
                       [R("qb", 128 * b, 128 * b + 128)], [R(oh, k * SEG + 1, (k + 1) * SEG)])
                op("V", lambda e: e.tensor_tensor_scan(T[sc][:, 0:nq * SEG], T.d0[:, 0:nq * SEG], T[oh][:, 0:nq * SEG], 0.0, MUL, ADD),
                   [R(oh), R("d0")], [R(sc)])
            ts(T.rqv[:], T.qb[:], 1.0 / 16, float(V - 1 - CAP * (r + 1)), MUL, ADD, [R("qb")], [R("rqv")])
            for b in range(2):
                sc = "sc%d" % b
                for k in range(nq):
                    bk, lo = 2 + 2 * b + k // 4, (k % 4) * CAP
                    op("T", lambda e: e.matmul(ps(bk, lo, lo + CAP), T.wa[:], T[sc][:, k * SEG + 1:(k + 1) * SEG], True, False), [R(sc), R("wa")], (), [bk])
                    op("T", lambda e: e.matmul(ps(bk, lo, lo + CAP), T.wb[:], T[sc][:, k * SEG:(k + 1) * SEG - 1], False, True), [R(sc), R("wb")], (), [bk])
            for b in range(2):
                for lo, hi, bk in ((0, na * CAP, 2 + 2 * b), (na * CAP, nq * CAP, 3 + 2 * b)):
                    if hi > lo:
                        act(T["rl%d" % b][:, lo:hi], ps(bk, 0, hi - lo), ACT.Relu, (), [R("rl%d" % b, lo, hi)], [bk])
            for b in range(2):
                rl = "rl%d" % b
                for k in range(nq):
                    op("T", lambda e: e.matmul(ps(6 + b, 0, CAP), T.idb[:], T[rl][:, k * CAP:(k + 1) * CAP], k == 0, k == nq - 1),
                       [R(rl, k * CAP, (k + 1) * CAP), R("idb")], (), [6 + b])
            if n == 0:
                convert()
            for b in range(2):
                lo, hi, zb = 128 * b, 128 * b + 128, 2 + 2 * b
                ts(T.yv[:, lo:hi], ps(6 + b, 0, CAP), 4096.0, -float(Z), MUL, ADD, (), [R("yv", lo, hi)], [6 + b])
                tt(ps(zb, 0, CAP), ps(6 + b, 0, CAP), T.rqv[:, lo:hi], ADD, [R("rqv")], [R("ps%d" % zb)], [6 + b, zb])
                tt(ps(zb, 0, CAP), ps(zb, 0, CAP), T.yv[:, lo:hi], MIN, [R("yv", lo, hi), R("ps%d" % zb)], [R("ps%d" % zb)], [zb])
                tt(T.zv[:, lo:hi], ps(zb, 0, CAP), T.xi[:], MAX, [R("xi"), R("ps%d" % zb)], [R("zv", lo, hi)], [zb])
                cp(T.o16[:, lo:hi], T.zv[:, lo:hi], [R("zv", lo, hi)], [R("o16", lo, hi)])
            LH = V + CAP * nq
            act(T.wl0[:, 0:LH].indirect(T.o16[:, 0:128]), T[E][:], ACT.Silu, [R(E), R("o16", 0, 128)], [R("wl0", 0, LH)])
            cp(T.wl1[:, 0:LH].indirect(T.o16[:, 128:256]), T[E][:], [R(E), R("o16", 128, 256)], [R("wl1", 0, LH)])
            before = [("lsq", total["lsq"])] if n else []
            for b in range(2):
                wl, items = "wl%d" % b, []
                for k in range(nq):
                    lo = V + CAP * k
                    items.append((T.rqb[k, b::2, :], T[wl][b::16, lo:lo + CAP], [R(wl, lo, lo + CAP)], ()))
                tok = dmas("S" if b == 0 else "Y", "dq%d" % b, items, before)
                need("G", tok[0], tok[1])
            to_later(lambda k: T.rqb[k], T.rland[r], "rq%d" % r, "lsq")
        elif n == 0:
            convert()
        for b in range(2):
            for k in range(4):
                bk, lo = 2 + k, 512 * k
                op("T", lambda e: e.matmul(ps(bk, 0, 512), T.sr[:, 128 * b:128 * b + 128], T[E][:, lo:lo + 512], True, True), [R("sr"), R(E, lo, lo + 512)], (), [bk])
                s = 1 if (k == 0 and r == 0) else 0
                c0 = Z + V * b + lo
                act(T.win[:, c0 + s:c0 + 512], ps(bk, s, 512), ACT.Copy, (), [R("win", c0 + s, c0 + 512)], [bk])
        for b in range(2):
            lo, hi = 128 * b, 128 * b + 128
            ts(T.u1[:, lo:hi], T.qb[:, lo:hi], 8.0, 1023.75 - V * r - 8.0 * V * r + Z + V * b + Z, MUL, ADD, [R("qb", lo, hi)], [R("u1", lo, hi)])
            ts(T.a1[:, lo:hi], T.qb[:, lo:hi], BW / 2048.0, float(BLK + Z + b - BW * r), MUL, ADD, [R("qb", lo, hi)], [R("a1", lo, hi)])
            tt(T.u1[:, lo:hi], ps(tw[b], 256, 384), T.u1[:, lo:hi], ADD, [R("u1", lo, hi)], [R("u1", lo, hi)], [tw[b]])
        tt(T.u1[:], T.u1[:], T.a1[:], MIN, [R("u1"), R("a1")], [R("u1")])
        if nq:
            for b in range(2):
                lo, hi = 128 * b, 128 * b + 128
                ts(T.si[:, lo:hi], ps(6 + b, 0, CAP), -1.0, 129.0, ADD, MUL, (), [R("si", lo, hi)], [6 + b])
            ts(T.si[:], T.si[:], 3, 254, AluOpType.arith_shift_right, AluOpType.bitwise_and, [R("si")], [R("si")])
            tt(T.av[:], T.yv[:], T.si[:], MIN, [R("yv"), R("si")], [R("av")])
            tt(T.av[:], T.av[:], T.u1[:], ADD, [R("av"), R("u1")], [R("av")])
        else:
            ts(T.av[:], T.u1[:], -float(Z), None, ADD, None, [R("u1")], [R("av")])
        cp(T.a16[:], T.av[:], [R("av")], [R("a16")])
        if n == 0 and nr:
            got = tokens("sra", sum(width(topo, cores, p) for p in range(nr)))
            cp(T.srf[:, 0:256 * nr], T.srl[:, 0:256 * nr], (), [R("srf", 0, 256 * nr)], (), [got])

        def gather(p):
            c0, c1 = 16 * p, 16 * p + 16
            arr = tokens("rq%d" % p, width(topo, cores, p))
            dmas("Y", "lw%d" % p, [(T.lq[:, c0:c1], T.rland[p], (), [R("lq", c0, c1)])], [arr])
            ts(T.lo[:, c0:c1], T.lq[:, c0:c1], 0.25 - V * r, None, ADD, None, [R("lq", c0, c1)], [R("lo", c0, c1)])
            cp(T.rpf[:, 16 * c0:16 * c1], T[E][:, 0:V].indirect(T.lo[:, c0:c1]), [R(E), R("lo", c0, c1)], [R("rpf", 16 * c0, 16 * c1)])
            bk = (0, 1, 6, 7)[p % 4]
            for b in range(2):
                m = 256 * p + 128 * b
                op("T", lambda e: e.matmul(T["ps%d" % bk][:, b:256:2], T.srf[:, m:m + 128], T.rpf[:, 256 * p + b:256 * p + 256:2], True, True),
                   [R("srf", m, m + 128), R("rpf", 16 * c0, 16 * c1)], (), [bk])

        def reply(p):
            lo, hi, bk = 256 * p, 256 * p + 256, (0, 1, 6, 7)[p % 4]
            left = [("ls%d" % p, total["ls%d" % p])] if n else []
            tok = cp(T.rp[:, lo:hi], ps(bk, 0, 256), (), [R("rp", lo, hi)], [bk], left)
            need("G", tok[0], tok[1])
            rid, pid, _s = topo.addr(cores[p])
            k = r - p - 1
            g.remote_dma(out_ap=T.ld[:, 256 * k:256 * k + 256], in_ap=T.rp[:, lo:hi], remote_sem=T.sem["rp%d" % r],
                         local_sem=T.sem["ls%d" % p], pid=pid, routing_id=rid, dma_engine_mask=rem_mask(pool))
            tokens("ls%d" % p, len(pool))
        if nr:
            gather(0)
            reply(0)
        for p in range(1, nr + 1):
            if p < nr:
                gather(p)
            if p > 1:
                reply(p - 1)
        for k, q in enumerate(later):
            arr = tokens("rp%d" % q, len(out_engines(topo, cores, q)))
            c0 = BLK + BW * (k + 1) + Z
            cp(T.win[:, c0:c0 + 256], T.ld[:, 256 * k:256 * k + 256], (), [R("win", c0, c0 + 256)], (), [arr])
        op("V", lambda e: e.tensor_tensor(T[X][:], T.win[:, 0:WC].indirect(T.a16[:, 0:128]), T[E][:], MAX), [R("win", 0, WC), R("a16"), R(E)], [R(X)])
        pieces = 1 if n < RO - 1 else PIECES
        for k in range(pieces):
            lo, hi = k * V // pieces, (k + 1) * V // pieces
            op("V", lambda e: e.tensor_tensor(T[X][:, lo:hi], T.win[:, 0:WC].indirect(T.a16[:, 128 + lo // 16:128 + hi // 16]), T[X][:, lo:hi], MAX),
               [R("win", 0, WC), R("a16"), R(X, lo, hi)], [R(X, lo, hi)])
            if n == RO - 1:
                dmas("Y" if k % 2 == 0 else "S", "st%d" % k, [(T.y[:, lo:hi], T[X][:, lo:hi], [R(X, lo, hi)], ())])
    for sem in sorted(total):
        need("G", sem, total[sem])
